import numpy as np
import ml_dtypes


def mxq(x, axis, fmt="e4m3"):
    dtype, down = {"e4m3": (ml_dtypes.float8_e4m3fn, 7), "e5m2": (ml_dtypes.float8_e5m2, 14)}[fmt]
    v = np.moveaxis(np.asarray(x, np.float32).astype(ml_dtypes.bfloat16).astype(np.float64), axis, -1)
    blocks = v.reshape(v.shape[:-1] + (-1, 32))
    amax = np.abs(blocks).max(-1, keepdims=True)
    byte = np.maximum(np.where(amax > 0, np.frexp(amax)[1] - 1 + 127, 0) - down, 1)
    scale = np.exp2(byte - 127.0)
    codes = (blocks / scale).astype(np.float32).astype(dtype).astype(np.float64)
    return np.moveaxis((codes * scale).reshape(v.shape), -1, axis)


WIDE = False


def mx_kscale(k):
    if not WIDE:
        return np.ones(k)
    levels = np.array([10, -10, 5, -5, 0])
    if k % 512:
        return np.exp2(np.random.permutation(np.resize(levels, k // 32))).repeat(32)
    a = np.empty((k // 512, 16))
    for p in range(k // 512):
        a[p, :8] = np.random.permutation(np.resize(levels, 8))
        for g in range(8):
            far = levels[np.abs(levels - a[p, g]) >= 10]
            a[p, g + 8] = far[np.random.randint(len(far))]
    return np.exp2(a.ravel()).repeat(32)


def f64(x):
    return np.asarray(x).astype(np.float64)


def striped(idx):
    return np.tile(idx.reshape(-1, 16).T, (8, 1)).astype(np.uint16)


def unstriped(offs):
    return offs[:16].T.reshape(-1).astype(np.int64)


E2M1 = np.array([0.0, 0.5, 1.0, 1.5, 2.0, 3.0, 4.0, 6.0, -0.0, -0.5, -1.0, -1.5, -2.0, -3.0, -4.0, -6.0])


def pack_weight(w, fmt):
    k, n = w.shape
    w = f64(np.asarray(w, np.float32).astype(ml_dtypes.bfloat16)).reshape(k // 32, 32, n)
    amax = np.abs(w).max(1)
    if fmt == "e4m3":
        byte = np.frexp(amax)[1] - 1 + 127 - 7
    else:
        mant, ex = np.frexp(amax / 6.0)
        byte = np.where(mant > 0.5, ex, ex - 1) + 127
    byte = np.clip(np.where(amax > 0, byte, 1), 1, 254)
    scaled = (w * np.exp2(127.0 - byte)[:, None, :]).reshape(k, n).astype(np.float32)
    by_word = np.ascontiguousarray(scaled.reshape(k // 512, 128, 4, n).transpose(0, 1, 3, 2))
    if fmt == "e4m3":
        words = by_word.astype(ml_dtypes.float8_e4m3fn).view(np.uint8)
    else:
        c = by_word.astype(ml_dtypes.float4_e2m1fn).view(np.uint8) & 0xF
        words = (c[..., 0::2] | (c[..., 1::2] << 4)).reshape(k // 512, 128, 2 * n)
    return np.ascontiguousarray(words), np.ascontiguousarray(byte.astype(np.uint8).reshape(k // 512, 16, n))


def unpack_weight(words, scales, fmt):
    g, _, n = scales.shape
    words = np.ascontiguousarray(words).reshape(g, 128, n, -1)
    if fmt == "e4m3":
        vals = words.view(ml_dtypes.float8_e4m3fn).astype(np.float64)
    else:
        nib = np.empty((g, 128, n, 4), np.uint8)
        nib[..., 0::2] = words & 0xF
        nib[..., 1::2] = words >> 4
        vals = E2M1[nib]
    vals = vals * np.repeat(np.exp2(scales.astype(np.float64) - 127.0), 8, axis=1)[..., None]
    return vals.transpose(0, 1, 3, 2).reshape(g * 512, n)


def gelu(v):
    return 0.5 * v * (1.0 + np.tanh(np.sqrt(2.0 / np.pi) * (v + 0.044715 * v**3)))


K, M, T, S = 1536, 128, 2048, 1024


def setup_inputs():
    n = np.random.standard_normal
    s = mx_kscale(K)[:, None]
    s2 = mx_kscale(512)[:, None]
    v = pack_weight(n((K, T)) * s, "e4m3")
    p_w4 = pack_weight(n((K, M)) / np.sqrt(K) / s, "e2m1")
    return {
        "tab_words": v[0],
        "tab_scales": v[1],
        "w4_words": p_w4[0],
        "w4_scales": p_w4[1],
        "c": (n((512, S)) * s2).astype(np.float32),
        "u": (n((512, M)) / np.sqrt(512) / s2).astype(np.float32),
        "ts": np.tile(np.exp(0.5 * n(T)), (128, 1)).astype(np.float32),
        "b": (0.3 * n(128)).astype(np.float32),
        "offs": striped(np.random.permutation(T)[:S]),
    }


def reference(tab_words, tab_scales, w4_words, w4_scales, c, u, ts, b, offs):
    tab_ = unpack_weight(tab_words, tab_scales, "e4m3")[:, unstriped(offs)]
    w4_ = unpack_weight(w4_words, w4_scales, "e2m1")
    c_ = mxq(f64(c), 0, "e4m3")
    u_ = mxq(f64(u), 0, "e4m3")
    y = w4_.T @ tab_ + u_.T @ c_
    y = y * f64(ts)[0][unstriped(offs)]
    return gelu(y + f64(b)[:, None])

@@ -1,0 +1,168 @@
+from contextlib import ExitStack
+
+import concourse.mybir as mybir
+from concourse.masks import make_identity
+
+K, M, T, S, L = 1536, 128, 2048, 1024, 512
+FLOPS = 2 * (K + L) * M * S
+
+F32 = mybir.dt.float32
+BF16 = mybir.dt.bfloat16
+I32 = mybir.dt.int32
+U32 = mybir.dt.uint32
+U16 = mybir.dt.uint16
+U8 = mybir.dt.uint8
+FP8X4 = mybir.dt.float8_e4m3fn_x4
+FP4X4 = mybir.dt.float4_e2m1fn_x4
+MULT = mybir.AluOpType.mult
+GELU = mybir.ActivationFunctionType.Gelu_apprx_tanh
+
+P = 128
+PACK = 4
+PASSES = K // (P * PACK)
+HALF = S // 2
+QUADS = 4
+ROWS = 16 * PASSES
+ROW0 = P - ROWS
+
+
+def tile_list_tabts_gelu_kernel(tc, tab_words, tab_scales, w4_words, w4_scales, c, u, ts, b, offs, out):
+    nc = tc.nc
+    with ExitStack() as ctx:
+        sb = ctx.enter_context(tc.tile_pool(name="sb", bufs=1))
+        ps = ctx.enter_context(tc.psum_pool(name="ps", bufs=1))
+
+        offsets = sb.tile([P, S // 16], U16, name="offsets")
+        nc.sync.dma_start(offsets[:], offs)
+
+        scale_win = sb.tile([P, T], U8, name="scale_win", tag="scales_then_words", align_bytes=64)
+        w4_planes = sb.tile([P, PASSES, M], U8, name="w4_planes", align_bytes=64)
+        tab_planes = sb.tile([P, PASSES, S], U8, name="tab_planes", align_bytes=64)
+        nc.vector.memset(scale_win[0:ROW0, :].bitcast(I32), 0)
+        nc.gpsimd.memset(w4_planes[:].rearrange("p a n -> p (a n)").bitcast(I32), 0)
+        nc.vector.memset(tab_planes[:].rearrange("p a n -> p (a n)").bitcast(I32), 0)
+
+        for a in range(PASSES):
+            nc.sync.dma_start(scale_win[ROW0 + a : ROW0 + ROWS : PASSES, :].bitcast(I32), tab_scales[a].bitcast(I32))
+
+        ts_cols = sb.tile([P, T // P], F32, name="ts_cols")
+        ident = sb.tile([P, P], F32, name="ident")
+        make_identity(nc, ident[:])
+        for q in range(QUADS):
+            nc.gpsimd.dma_start(
+                w4_planes[32 * q : 32 * q + 4, :, :].bitcast(I32),
+                w4_scales[:, 4 * q : 4 * q + 4, :].rearrange("a r n -> r a n").bitcast(I32),
+            )
+
+        def load_words(a, tag):
+            win = sb.tile([P, T], I32, name=f"word_win{a}", tag=tag, align_bytes=64)
+            nc.sync.dma_start(win[:], tab_words[a].rearrange("p t i -> p (t i)").bitcast(I32))
+            return win
+
+        def load_rows(rows, name, tag):
+            raw = sb.tile([P, PACK, rows.shape[1]], F32, name=name, tag=tag, align_bytes=64)
+            nc.sync.dma_start(raw[:], rows.rearrange("(p i) w -> p i w", i=PACK))
+            return raw
+
+        w4_codes = sb.tile([P, PASSES, 2 * M], U8, name="w4_codes", align_bytes=64)
+        bias = sb.tile([P, 1], F32, name="bias")
+        c_cuts = [(0, 512), (512, 768), (768, 1024)]
+
+        nc.sync.dma_start(ts_cols[:], ts[0:1, :].rearrange("o (p c) -> (o p) c", p=P))
+        word_win = [load_words(0, "words_then_c")]
+        nc.sync.dma_start(w4_codes[:].bitcast(I32), w4_words.rearrange("a p n -> p a n").bitcast(I32))
+        nc.sync.dma_start(bias[:], b.rearrange("(p o) -> p o", o=1))
+        word_win.append(load_words(1, "words1"))
+        u_raw = load_rows(u, "u_raw", "u_raw")
+        c_raw = [load_rows(c[:, lo:hi], f"c_raw{lo}", f"c_raw{lo}") for lo, hi in c_cuts[:2]]
+
+        ts_win = sb.tile([P, T], F32, name="ts_win")
+        ts_view = ts_win[:].rearrange("p (q c) -> p q c", q=P)
+        for g in range(T // P // 4):
+            spread = ps.tile([P, 4, P], F32, name=f"spread{g}")
+            for k in range(4):
+                col = 4 * g + k
+                nc.tensor.transpose(spread[:, k, :], ts_cols[:, col : col + 1].to_broadcast([P, P]), ident[:])
+            nc.scalar.copy(ts_view[:, :, 4 * g : 4 * g + 4], spread[:].rearrange("p k q -> p q k"))
+
+        def interleave(raw, name):
+            grouped = sb.tile([P, raw.shape[2], PACK], BF16, name=name, align_bytes=64)
+            nc.scalar.copy(
+                grouped[:].rearrange("p (w e) i -> p w i e", e=4), raw[:].rearrange("p i (w e) -> p w i e", e=4)
+            )
+            return grouped
+
+        def quantize(grouped, name):
+            width = grouped.shape[1]
+            codes = sb.tile([P, width], U32, name=name + "_codes", align_bytes=64)
+            scales = sb.tile([P, width], U8, name=name + "_scales", align_bytes=64)
+            nc.vector.quantize_mx(out=codes[:].bitcast(FP8X4), scales=scales[:], in_=grouped[:].rearrange("p w i -> p (w i)"))
+            return codes, scales
+
+        def gather(dst, window, lo, hi):
+            nc.vector.tensor_copy(dst, window.indirect(offsets[:, lo // 16 : hi // 16]))
+
+        picked = [sb.tile([P, S], U32, name=f"picked{a}", align_bytes=64) for a in range(PASSES - 1)]
+        last = [sb.tile([P, HALF], U32, name=f"last{h}", align_bytes=64) for h in range(2)]
+        picked_scales = sb.tile([P, S], U8, name="picked_scales", align_bytes=64)
+        ts_picked = sb.tile([P, S], F32, name="ts_picked")
+
+        gather(picked_scales[:], scale_win[:], 0, S)
+        for q in range(QUADS):
+            nc.sync.dma_start(
+                tab_planes[32 * q : 32 * q + 4, :, :].bitcast(I32),
+                picked_scales[ROW0 + 12 * q : ROW0 + 12 * q + 12, :].bitcast(I32),
+            )
+        word_win.append(load_words(2, "scales_then_words"))
+        gather(picked[0][:], word_win[0][:].bitcast(U32), 0, S)
+        c_raw.append(load_rows(c[:, c_cuts[2][0] : c_cuts[2][1]], "c_raw_last", "words_then_c"))
+        gather(picked[1][:], word_win[1][:].bitcast(U32), 0, S)
+        gather(ts_picked[:], ts_win[:], 0, S)
+        u_codes, u_scales = quantize(interleave(u_raw, "u_bf"), "u")
+        c_q = [quantize(interleave(c_raw[k], f"c_bf{k}"), f"c{k}") for k in range(2)]
+        for h in range(2):
+            gather(last[h][:], word_win[2][:].bitcast(U32), h * HALF, (h + 1) * HALF)
+        c_q.append(quantize(interleave(c_raw[2], "c_bf2"), "c2"))
+
+        acc = [ps.tile([P, HALF], F32, name=f"acc{h}") for h in range(2)]
+
+        def table_pass(h, a, words):
+            nc.tensor.matmul_mx(
+                out=acc[h][:],
+                lhsT=w4_codes[:, a, :].bitcast(FP4X4),
+                lhsT_scale=w4_planes[:, a, :],
+                rhs=words.bitcast(FP8X4),
+                rhs_scale=tab_planes[:, a, h * HALF : (h + 1) * HALF],
+                start=(a == 0),
+                stop=(a == PASSES - 1 and h == 0),
+            )
+
+        def c_pass(k):
+            lo, hi = c_cuts[k]
+            h = lo // HALF
+            nc.tensor.matmul_mx(
+                out=acc[h][:, lo - h * HALF : hi - h * HALF],
+                lhsT=u_codes[:].bitcast(FP8X4),
+                lhsT_scale=u_scales[:],
+                rhs=c_q[k][0][:].bitcast(FP8X4),
+                rhs_scale=c_q[k][1][:],
+                start=False,
+                stop=(k == 2),
+            )
+
+        for a in range(PASSES - 1):
+            for h in range(2):
+                table_pass(h, a, picked[a][:, h * HALF : (h + 1) * HALF])
+        for k in range(2):
+            c_pass(k)
+        for h in range(2):
+            table_pass(h, PASSES - 1, last[h][:])
+        c_pass(2)
+
+        for k, (lo, hi) in enumerate(c_cuts):
+            h = lo // HALF
+            scaled = sb.tile([P, hi - lo], F32, name=f"scaled{k}")
+            nc.vector.tensor_tensor(scaled[:], acc[h][:, lo - h * HALF : hi - h * HALF], ts_picked[:, lo:hi], MULT)
+            result = sb.tile([P, hi - lo], F32, name=f"result{k}")
+            nc.scalar.activation(result[:], scaled[:], GELU, bias=bias[:])
+            nc.sync.dma_start(out[:, lo:hi], result[:])

@@ -39,8 +39,6 @@ def tile_list_tabts_gelu_kernel(tc, tab_words, tab_scales, w4_words, w4_scales, 
         w4_planes = sb.tile([P, PASSES, M], U8, name="w4_planes", align_bytes=64)
         tab_planes = sb.tile([P, PASSES, S], U8, name="tab_planes", align_bytes=64)
         nc.vector.memset(scale_win[0:ROW0, :].bitcast(I32), 0)
-        nc.gpsimd.memset(w4_planes[:].rearrange("p a n -> p (a n)").bitcast(I32), 0)
-        nc.vector.memset(tab_planes[:].rearrange("p a n -> p (a n)").bitcast(I32), 0)
 
         for a in range(PASSES):
             nc.sync.dma_start(scale_win[ROW0 + a : ROW0 + ROWS : PASSES, :].bitcast(I32), tab_scales[a].bitcast(I32))
@@ -48,11 +46,6 @@ def tile_list_tabts_gelu_kernel(tc, tab_words, tab_scales, w4_words, w4_scales, 
         ts_cols = sb.tile([P, T // P], F32, name="ts_cols")
         ident = sb.tile([P, P], F32, name="ident")
         make_identity(nc, ident[:])
-        for q in range(QUADS):
-            nc.gpsimd.dma_start(
-                w4_planes[32 * q : 32 * q + 4, :, :].bitcast(I32),
-                w4_scales[:, 4 * q : 4 * q + 4, :].rearrange("a r n -> r a n").bitcast(I32),
-            )
 
         def load_words(a, tag):
             win = sb.tile([P, T], I32, name=f"word_win{a}", tag=tag, align_bytes=64)
@@ -68,13 +61,18 @@ def tile_list_tabts_gelu_kernel(tc, tab_words, tab_scales, w4_words, w4_scales, 
         bias = sb.tile([P, 1], F32, name="bias")
         c_cuts = [(0, 512), (512, 768), (768, 1024)]
 
-        nc.sync.dma_start(ts_cols[:], ts[0:1, :].rearrange("o (p c) -> (o p) c", p=P))
-        word_win = [load_words(0, "words_then_c")]
-        nc.sync.dma_start(w4_codes[:].bitcast(I32), w4_words.rearrange("a p n -> p a n").bitcast(I32))
+        nc.scalar.dma_start(ts_cols[:], ts[0:1, :].rearrange("o (p c) -> (o p) c", p=P))
+        word_win = [load_words(0, "words0_then_c")]
         nc.sync.dma_start(bias[:], b.rearrange("(p o) -> p o", o=1))
-        word_win.append(load_words(1, "words1"))
+        for q in range(QUADS):
+            nc.sync.dma_start(
+                w4_planes[32 * q : 32 * q + 4, :, :].bitcast(I32),
+                w4_scales[:, 4 * q : 4 * q + 4, :].rearrange("a r n -> r a n").bitcast(I32),
+            )
+        word_win.append(load_words(1, "words1_then_c"))
+        nc.sync.dma_start(w4_codes[:].bitcast(I32), w4_words.rearrange("a p n -> p a n").bitcast(I32))
         u_raw = load_rows(u, "u_raw", "u_raw")
-        c_raw = [load_rows(c[:, lo:hi], f"c_raw{lo}", f"c_raw{lo}") for lo, hi in c_cuts[:2]]
+        c_raw = [load_rows(c[:, c_cuts[0][0] : c_cuts[0][1]], "c_raw0", "c_raw0")]
 
         ts_win = sb.tile([P, T], F32, name="ts_win")
         ts_view = ts_win[:].rearrange("p (q c) -> p q c", q=P)
@@ -85,9 +83,9 @@ def tile_list_tabts_gelu_kernel(tc, tab_words, tab_scales, w4_words, w4_scales, 
                 nc.tensor.transpose(spread[:, k, :], ts_cols[:, col : col + 1].to_broadcast([P, P]), ident[:])
             nc.scalar.copy(ts_view[:, :, 4 * g : 4 * g + 4], spread[:].rearrange("p k q -> p q k"))
 
-        def interleave(raw, name):
+        def interleave(raw, name, copy):
             grouped = sb.tile([P, raw.shape[2], PACK], BF16, name=name, align_bytes=64)
-            nc.scalar.copy(
+            copy(
                 grouped[:].rearrange("p (w e) i -> p w i e", e=4), raw[:].rearrange("p i (w e) -> p w i e", e=4)
             )
             return grouped
@@ -115,54 +113,60 @@ def tile_list_tabts_gelu_kernel(tc, tab_words, tab_scales, w4_words, w4_scales, 
             )
         word_win.append(load_words(2, "scales_then_words"))
         gather(picked[0][:], word_win[0][:].bitcast(U32), 0, S)
-        c_raw.append(load_rows(c[:, c_cuts[2][0] : c_cuts[2][1]], "c_raw_last", "words_then_c"))
+        c_raw.append(load_rows(c[:, c_cuts[1][0] : c_cuts[1][1]], "c_raw1", "words0_then_c"))
         gather(picked[1][:], word_win[1][:].bitcast(U32), 0, S)
+        c_raw.append(load_rows(c[:, c_cuts[2][0] : c_cuts[2][1]], "c_raw2", "words1_then_c"))
         gather(ts_picked[:], ts_win[:], 0, S)
-        u_codes, u_scales = quantize(interleave(u_raw, "u_bf"), "u")
-        c_q = [quantize(interleave(c_raw[k], f"c_bf{k}"), f"c{k}") for k in range(2)]
+        u_codes, u_scales = quantize(interleave(u_raw, "u_bf", nc.scalar.copy), "u")
+        c_q = [quantize(interleave(c_raw[0], "c_bf0", nc.scalar.copy), "c0")]
         for h in range(2):
             gather(last[h][:], word_win[2][:].bitcast(U32), h * HALF, (h + 1) * HALF)
-        c_q.append(quantize(interleave(c_raw[2], "c_bf2"), "c2"))
+        c_q.append(quantize(interleave(c_raw[1], "c_bf1", nc.scalar.copy), "c1"))
+        c_q.append(quantize(interleave(c_raw[2], "c_bf2", nc.vector.tensor_copy), "c2"))
 
-        acc = [ps.tile([P, HALF], F32, name=f"acc{h}") for h in range(2)]
+        acc = [ps.tile([P, hi - lo], F32, name=f"acc{lo}") for lo, hi in c_cuts]
 
-        def table_pass(h, a, words):
-            nc.tensor.matmul_mx(
-                out=acc[h][:],
-                lhsT=w4_codes[:, a, :].bitcast(FP4X4),
-                lhsT_scale=w4_planes[:, a, :],
-                rhs=words.bitcast(FP8X4),
-                rhs_scale=tab_planes[:, a, h * HALF : (h + 1) * HALF],
-                start=(a == 0),
-                stop=(a == PASSES - 1 and h == 0),
-            )
+        def table_pass(k, a):
+            lo, hi = c_cuts[k]
+            step = 512 if hi - lo == 512 else 128
+            for n0 in range(lo, hi, step):
+                if a < PASSES - 1:
+                    words = picked[a][:, n0 : n0 + step]
+                else:
+                    words = last[n0 // HALF][:, n0 % HALF : n0 % HALF + step]
+                nc.tensor.matmul_mx(
+                    out=acc[k][:, n0 - lo : n0 - lo + step],
+                    lhsT=w4_codes[:, a, :].bitcast(FP4X4),
+                    lhsT_scale=w4_planes[:, a, :],
+                    rhs=words.bitcast(FP8X4),
+                    rhs_scale=tab_planes[:, a, n0 : n0 + step],
+                    start=(a == 0 and n0 == lo),
+                    stop=(a == PASSES - 1 and k == 0),
+                )
 
         def c_pass(k):
-            lo, hi = c_cuts[k]
-            h = lo // HALF
             nc.tensor.matmul_mx(
-                out=acc[h][:, lo - h * HALF : hi - h * HALF],
+                out=acc[k][:],
                 lhsT=u_codes[:].bitcast(FP8X4),
                 lhsT_scale=u_scales[:],
                 rhs=c_q[k][0][:].bitcast(FP8X4),
                 rhs_scale=c_q[k][1][:],
                 start=False,
-                stop=(k == 2),
+                stop=(k > 0),
             )
 
         for a in range(PASSES - 1):
-            for h in range(2):
-                table_pass(h, a, picked[a][:, h * HALF : (h + 1) * HALF])
-        for k in range(2):
-            c_pass(k)
-        for h in range(2):
-            table_pass(h, PASSES - 1, last[h][:])
+            for k in range(3):
+                table_pass(k, a)
+        c_pass(0)
+        for k in range(3):
+            table_pass(k, PASSES - 1)
+        c_pass(1)
         c_pass(2)
 
         for k, (lo, hi) in enumerate(c_cuts):
-            h = lo // HALF
-            scaled = sb.tile([P, hi - lo], F32, name=f"scaled{k}")
-            nc.vector.tensor_tensor(scaled[:], acc[h][:, lo - h * HALF : hi - h * HALF], ts_picked[:, lo:hi], MULT)
+            scaled = sb.tile([P, hi - lo], F32, name=f"scaled{k}", tag=("c_bf2" if k == 1 else f"scaled{k}"), align_bytes=64)
+            nc.vector.tensor_tensor(scaled[:], acc[k][:], ts_picked[:, lo:hi], MULT)
             result = sb.tile([P, hi - lo], F32, name=f"result{k}")
             nc.scalar.activation(result[:], scaled[:], GELU, bias=bias[:])
             nc.sync.dma_start(out[:, lo:hi], result[:])

@@ -23,7 +23,7 @@ PASSES = K // (P * PACK)
 HALF = S // 2
 QUADS = 4
 ROWS = 16 * PASSES
-ROW0 = P - ROWS
+ROW0 = 48
 
 
 def tile_list_tabts_gelu_kernel(tc, tab_words, tab_scales, w4_words, w4_scales, c, u, ts, b, offs, out):
@@ -39,6 +39,7 @@ def tile_list_tabts_gelu_kernel(tc, tab_words, tab_scales, w4_words, w4_scales, 
         w4_planes = sb.tile([P, PASSES, M], U8, name="w4_planes", align_bytes=64)
         tab_planes = sb.tile([P, PASSES, S], U8, name="tab_planes", align_bytes=64)
         nc.vector.memset(scale_win[0:ROW0, :].bitcast(I32), 0)
+        nc.vector.memset(scale_win[ROW0 + ROWS : P, :].bitcast(I32), 0)
 
         for a in range(PASSES):
             nc.sync.dma_start(scale_win[ROW0 + a : ROW0 + ROWS : PASSES, :].bitcast(I32), tab_scales[a].bitcast(I32))
@@ -58,12 +59,10 @@ def tile_list_tabts_gelu_kernel(tc, tab_words, tab_scales, w4_words, w4_scales, 
             return raw
 
         w4_codes = sb.tile([P, PASSES, 2 * M], U8, name="w4_codes", align_bytes=64)
-        bias = sb.tile([P, 1], F32, name="bias")
-        c_cuts = [(0, 512), (512, 768), (768, 1024)]
+        c_cuts = [(0, 512), (512, 768), (768, 896), (896, 1024)]
 
         nc.scalar.dma_start(ts_cols[:], ts[0:1, :].rearrange("o (p c) -> (o p) c", p=P))
         word_win = [load_words(0, "words0_then_c")]
-        nc.sync.dma_start(bias[:], b.rearrange("(p o) -> p o", o=1))
         for q in range(QUADS):
             nc.sync.dma_start(
                 w4_planes[32 * q : 32 * q + 4, :, :].bitcast(I32),
@@ -101,12 +100,11 @@ def tile_list_tabts_gelu_kernel(tc, tab_words, tab_scales, w4_words, w4_scales, 
             nc.vector.tensor_copy(dst, window.indirect(offsets[:, lo // 16 : hi // 16]))
 
         picked = [sb.tile([P, S], U32, name=f"picked{a}", align_bytes=64) for a in range(PASSES - 1)]
-        last = [sb.tile([P, HALF], U32, name=f"last{h}", align_bytes=64) for h in range(2)]
-        picked_scales = sb.tile([P, S], U8, name="picked_scales", align_bytes=64)
+        picked_scales = sb.tile([P, S], U8, name="picked_scales", tag="picked_scales_then_bias", align_bytes=64)
         ts_picked = sb.tile([P, S], F32, name="ts_picked")
 
         gather(picked_scales[:], scale_win[:], 0, S)
-        for q in range(QUADS):
+        for q in (0, 2, 1, 3):
             nc.sync.dma_start(
                 tab_planes[32 * q : 32 * q + 4, :, :].bitcast(I32),
                 picked_scales[ROW0 + 12 * q : ROW0 + 12 * q + 12, :].bitcast(I32),
@@ -116,13 +114,22 @@ def tile_list_tabts_gelu_kernel(tc, tab_words, tab_scales, w4_words, w4_scales, 
         c_raw.append(load_rows(c[:, c_cuts[1][0] : c_cuts[1][1]], "c_raw1", "words0_then_c"))
         gather(picked[1][:], word_win[1][:].bitcast(U32), 0, S)
         c_raw.append(load_rows(c[:, c_cuts[2][0] : c_cuts[2][1]], "c_raw2", "words1_then_c"))
+        bias = sb.tile([P, 1], F32, name="bias", tag="picked_scales_then_bias", align_bytes=64)
+        nc.sync.dma_start(bias[:], b.rearrange("(p o) -> p o", o=1))
         gather(ts_picked[:], ts_win[:], 0, S)
         u_codes, u_scales = quantize(interleave(u_raw, "u_bf", nc.scalar.copy), "u")
+        c_raw.append(load_rows(c[:, c_cuts[3][0] : c_cuts[3][1]], "c_raw3", "u_raw"))
         c_q = [quantize(interleave(c_raw[0], "c_bf0", nc.scalar.copy), "c0")]
+        last = [
+            sb.tile([P, HALF], U32, name=f"last{h}", tag=("c_bf0" if h == 0 else "last1"), align_bytes=64) for h in range(2)
+        ]
         for h in range(2):
             gather(last[h][:], word_win[2][:].bitcast(U32), h * HALF, (h + 1) * HALF)
         c_q.append(quantize(interleave(c_raw[1], "c_bf1", nc.scalar.copy), "c1"))
-        c_q.append(quantize(interleave(c_raw[2], "c_bf2", nc.vector.tensor_copy), "c2"))
+        c_bf2 = interleave(c_raw[2], "c_bf2", nc.scalar.copy)
+        c_bf3 = interleave(c_raw[3], "c_bf3", nc.vector.tensor_copy)
+        c_q.append(quantize(c_bf2, "c2"))
+        c_q.append(quantize(c_bf3, "c3"))
 
         acc = [ps.tile([P, hi - lo], F32, name=f"acc{lo}") for lo, hi in c_cuts]
 
@@ -156,16 +163,17 @@ def tile_list_tabts_gelu_kernel(tc, tab_words, tab_scales, w4_words, w4_scales, 
             )
 
         for a in range(PASSES - 1):
-            for k in range(3):
+            for k in range(4):
                 table_pass(k, a)
         c_pass(0)
-        for k in range(3):
+        for k in range(4):
             table_pass(k, PASSES - 1)
         c_pass(1)
         c_pass(2)
+        c_pass(3)
 
         for k, (lo, hi) in enumerate(c_cuts):
-            scaled = sb.tile([P, hi - lo], F32, name=f"scaled{k}", tag=("c_bf2" if k == 1 else f"scaled{k}"), align_bytes=64)
+            scaled = sb.tile([P, hi - lo], F32, name=f"scaled{k}", tag=("c_bf3" if k == 1 else f"scaled{k}"), align_bytes=64)
             nc.vector.tensor_tensor(scaled[:], acc[k][:], ts_picked[:, lo:hi], MULT)
             result = sb.tile([P, hi - lo], F32, name=f"result{k}")
             nc.scalar.activation(result[:], scaled[:], GELU, bias=bias[:])

@@ -35,7 +35,7 @@ def tile_list_tabts_gelu_kernel(tc, tab_words, tab_scales, w4_words, w4_scales, 
         offsets = sb.tile([P, S // 16], U16, name="offsets")
         nc.sync.dma_start(offsets[:], offs)
 
-        scale_win = sb.tile([P, T], U8, name="scale_win", tag="scales_then_words", align_bytes=64)
+        scale_win = sb.tile([P, T], U8, name="scale_win", tag="scales_then_c", align_bytes=64)
         w4_planes = sb.tile([P, PASSES, M], U8, name="w4_planes", align_bytes=64)
         tab_planes = sb.tile([P, PASSES, S], U8, name="tab_planes", align_bytes=64)
         nc.vector.memset(scale_win[0:ROW0, :].bitcast(I32), 0)
@@ -68,10 +68,11 @@ def tile_list_tabts_gelu_kernel(tc, tab_words, tab_scales, w4_words, w4_scales, 
                 w4_planes[32 * q : 32 * q + 4, :, :].bitcast(I32),
                 w4_scales[:, 4 * q : 4 * q + 4, :].rearrange("a r n -> r a n").bitcast(I32),
             )
-        word_win.append(load_words(1, "words1_then_c"))
         nc.sync.dma_start(w4_codes[:].bitcast(I32), w4_words.rearrange("a p n -> p a n").bitcast(I32))
         u_raw = load_rows(u, "u_raw", "u_raw")
         c_raw = [load_rows(c[:, c_cuts[0][0] : c_cuts[0][1]], "c_raw0", "c_raw0")]
+        word_win.append(load_words(1, "words1"))
+        word_win.append(load_words(2, "words2"))
 
         ts_win = sb.tile([P, T], F32, name="ts_win")
         ts_view = ts_win[:].rearrange("p (q c) -> p q c", q=P)
@@ -109,20 +110,17 @@ def tile_list_tabts_gelu_kernel(tc, tab_words, tab_scales, w4_words, w4_scales, 
                 tab_planes[32 * q : 32 * q + 4, :, :].bitcast(I32),
                 picked_scales[ROW0 + 12 * q : ROW0 + 12 * q + 12, :].bitcast(I32),
             )
-        word_win.append(load_words(2, "scales_then_words"))
+        c_raw.append(load_rows(c[:, c_cuts[1][0] : c_cuts[1][1]], "c_raw1", "scales_then_c"))
         gather(picked[0][:], word_win[0][:].bitcast(U32), 0, S)
-        c_raw.append(load_rows(c[:, c_cuts[1][0] : c_cuts[1][1]], "c_raw1", "words0_then_c"))
-        gather(picked[1][:], word_win[1][:].bitcast(U32), 0, S)
-        c_raw.append(load_rows(c[:, c_cuts[2][0] : c_cuts[2][1]], "c_raw2", "words1_then_c"))
+        c_raw.append(load_rows(c[:, c_cuts[2][0] : c_cuts[2][1]], "c_raw2", "words0_then_c"))
         bias = sb.tile([P, 1], F32, name="bias", tag="picked_scales_then_bias", align_bytes=64)
         nc.sync.dma_start(bias[:], b.rearrange("(p o) -> p o", o=1))
         gather(ts_picked[:], ts_win[:], 0, S)
         u_codes, u_scales = quantize(interleave(u_raw, "u_bf", nc.scalar.copy), "u")
         c_raw.append(load_rows(c[:, c_cuts[3][0] : c_cuts[3][1]], "c_raw3", "u_raw"))
+        gather(picked[1][:], word_win[1][:].bitcast(U32), 0, S)
         c_q = [quantize(interleave(c_raw[0], "c_bf0", nc.scalar.copy), "c0")]
-        last = [
-            sb.tile([P, HALF], U32, name=f"last{h}", tag=("c_bf0" if h == 0 else "last1"), align_bytes=64) for h in range(2)
-        ]
+        last = [sb.tile([P, HALF], U32, name=f"last{h}", align_bytes=64) for h in range(2)]
         for h in range(2):
             gather(last[h][:], word_win[2][:].bitcast(U32), h * HALF, (h + 1) * HALF)
         c_q.append(quantize(interleave(c_raw[1], "c_bf1", nc.scalar.copy), "c1"))
@@ -147,7 +145,7 @@ def tile_list_tabts_gelu_kernel(tc, tab_words, tab_scales, w4_words, w4_scales, 
                     lhsT_scale=w4_planes[:, a, :],
                     rhs=words.bitcast(FP8X4),
                     rhs_scale=tab_planes[:, a, n0 : n0 + step],
-                    start=(a == 0 and n0 == lo),
+                    start=(a == 0 and n0 == lo and k > 0),
                     stop=(a == PASSES - 1 and k == 0),
                 )
 
@@ -158,19 +156,22 @@ def tile_list_tabts_gelu_kernel(tc, tab_words, tab_scales, w4_words, w4_scales, 
                 lhsT_scale=u_scales[:],
                 rhs=c_q[k][0][:].bitcast(FP8X4),
                 rhs_scale=c_q[k][1][:],
-                start=False,
+                start=(k == 0),
                 stop=(k > 0),
             )
 
-        for a in range(PASSES - 1):
-            for k in range(4):
-                table_pass(k, a)
         c_pass(0)
-        for k in range(4):
-            table_pass(k, PASSES - 1)
+        for a in range(PASSES):
+            table_pass(0, a)
+        for a in range(PASSES - 1):
+            for k in range(1, 4):
+                table_pass(k, a)
+        table_pass(1, PASSES - 1)
         c_pass(1)
-        c_pass(2)
-        c_pass(3)
+        for k in range(2, 4):
+            table_pass(k, PASSES - 1)
+        for k in range(2, 4):
+            c_pass(k)
 
         for k, (lo, hi) in enumerate(c_cuts):
             scaled = sb.tile([P, hi - lo], F32, name=f"scaled{k}", tag=("c_bf3" if k == 1 else f"scaled{k}"), align_bytes=64)

@@ -47,6 +47,8 @@ def tile_list_tabts_gelu_kernel(tc, tab_words, tab_scales, w4_words, w4_scales, 
         ts_cols = sb.tile([P, T // P], F32, name="ts_cols")
         ident = sb.tile([P, P], F32, name="ident")
         make_identity(nc, ident[:])
+        warm = sb.tile([P, 1], F32, name="warm")
+        nc.scalar.activation(warm[:], ident[:, 0:1], GELU)
 
         def load_words(a, tag):
             win = sb.tile([P, T], I32, name=f"word_win{a}", tag=tag, align_bytes=64)

@@ -22,74 +22,70 @@ PACK = 4
 PASSES = K // (P * PACK)
 HALF = S // 2
 QUADS = 4
-ROWS = 16 * PASSES
-ROW0 = 48
+ROW0 = 36
+WIN0 = 4 * T
+TS_ROW = P - 1
 
 
 def tile_list_tabts_gelu_kernel(tc, tab_words, tab_scales, w4_words, w4_scales, c, u, ts, b, offs, out):
     nc = tc.nc
     with ExitStack() as ctx:
         sb = ctx.enter_context(tc.tile_pool(name="sb", bufs=1))
+        shared = ctx.enter_context(tc.tile_pool(name="shared", bufs=1))
+        shared_u = ctx.enter_context(tc.tile_pool(name="shared_u", bufs=1))
         ps = ctx.enter_context(tc.psum_pool(name="ps", bufs=1))
+
+        c_cuts = [(0, 256), (256, 512), (512, 768), (768, 896), (896, 1024)]
 
         offsets = sb.tile([P, S // 16], U16, name="offsets")
         nc.sync.dma_start(offsets[:], offs)
 
-        scale_win = sb.tile([P, T], U8, name="scale_win", tag="scales_then_c", align_bytes=64)
-        w4_planes = sb.tile([P, PASSES, M], U8, name="w4_planes", align_bytes=64)
-        tab_planes = sb.tile([P, PASSES, S], U8, name="tab_planes", align_bytes=64)
-        nc.vector.memset(scale_win[0:ROW0, :].bitcast(I32), 0)
-        nc.vector.memset(scale_win[ROW0 + ROWS : P, :].bitcast(I32), 0)
+        scale_win = shared.tile([P, T], U8, name="scale_win", offset=4096 - T // 2, align_bytes=64)
+        nc.vector.memset(scale_win[:].bitcast(I32), 0)
+        ts_win = sb.tile([P, T], F32, name="ts_win", align_bytes=64)
+        nc.vector.memset(ts_win[0:TS_ROW, 0 : T // 2].bitcast(I32), 0)
+        nc.gpsimd.memset(ts_win[0:TS_ROW, T // 2 : T].bitcast(I32), 0)
+        nc.scalar.dma_start(ts_win[TS_ROW:P, :], ts[0:1, :])
 
-        for a in range(PASSES):
-            nc.sync.dma_start(scale_win[ROW0 + a : ROW0 + ROWS : PASSES, :].bitcast(I32), tab_scales[a].bitcast(I32))
-
-        ts_cols = sb.tile([P, T // P], F32, name="ts_cols")
         ident = sb.tile([P, P], F32, name="ident")
         make_identity(nc, ident[:])
         warm = sb.tile([P, 1], F32, name="warm")
         nc.scalar.activation(warm[:], ident[:, 0:1], GELU)
 
-        def load_words(a, tag):
-            win = sb.tile([P, T], I32, name=f"word_win{a}", tag=tag, align_bytes=64)
+        def load_words(a, win):
             nc.sync.dma_start(win[:], tab_words[a].rearrange("p t i -> p (t i)").bitcast(I32))
             return win
 
-        def load_rows(rows, name, tag):
-            raw = sb.tile([P, PACK, rows.shape[1]], F32, name=name, tag=tag, align_bytes=64)
+        def load_rows(rows, raw):
             nc.sync.dma_start(raw[:], rows.rearrange("(p i) w -> p i w", i=PACK))
             return raw
 
-        w4_codes = sb.tile([P, PASSES, 2 * M], U8, name="w4_codes", align_bytes=64)
-        c_cuts = [(0, 512), (512, 768), (768, 896), (896, 1024)]
+        def load_chunk(k, pool, offset):
+            lo, hi = c_cuts[k]
+            raw = pool.tile([P, PACK, hi - lo], F32, name=f"c_raw{k}", offset=offset, align_bytes=64)
+            return load_rows(c[:, lo:hi], raw)
 
-        nc.scalar.dma_start(ts_cols[:], ts[0:1, :].rearrange("o (p c) -> (o p) c", p=P))
-        word_win = [load_words(0, "words0_then_c")]
+        w4_planes = sb.tile([P, PASSES, M], U8, name="w4_planes", align_bytes=64)
+        w4_codes = sb.tile([P, PASSES, 2 * M], U8, name="w4_codes", align_bytes=64)
+
+        word_win = [load_words(0, shared.tile([P, T], I32, name="word_win0", offset=WIN0, align_bytes=64))]
+        for a in range(PASSES):
+            first = ROW0 + 4 * a
+            nc.sync.dma_start(scale_win[first : first + 46 : 3, :].bitcast(I32), tab_scales[a].bitcast(I32))
+        u_raw = load_rows(u, shared_u.tile([P, PACK, M], F32, name="u_raw", offset=0, align_bytes=64))
+        nc.sync.dma_start(w4_codes[:].bitcast(I32), w4_words.rearrange("a p n -> p a n").bitcast(I32))
+        word_win.append(load_words(1, sb.tile([P, T], I32, name="word_win1", tag="words1_then_bias", align_bytes=64)))
         for q in range(QUADS):
             nc.sync.dma_start(
                 w4_planes[32 * q : 32 * q + 4, :, :].bitcast(I32),
                 w4_scales[:, 4 * q : 4 * q + 4, :].rearrange("a r n -> r a n").bitcast(I32),
             )
-        nc.sync.dma_start(w4_codes[:].bitcast(I32), w4_words.rearrange("a p n -> p a n").bitcast(I32))
-        u_raw = load_rows(u, "u_raw", "u_raw")
-        c_raw = [load_rows(c[:, c_cuts[0][0] : c_cuts[0][1]], "c_raw0", "c_raw0")]
-        word_win.append(load_words(1, "words1"))
-        word_win.append(load_words(2, "words2"))
-
-        ts_win = sb.tile([P, T], F32, name="ts_win")
-        ts_view = ts_win[:].rearrange("p (q c) -> p q c", q=P)
-        for g in range(T // P // 4):
-            spread = ps.tile([P, 4, P], F32, name=f"spread{g}")
-            for k in range(4):
-                col = 4 * g + k
-                nc.tensor.transpose(spread[:, k, :], ts_cols[:, col : col + 1].to_broadcast([P, P]), ident[:])
-            nc.scalar.copy(ts_view[:, :, 4 * g : 4 * g + 4], spread[:].rearrange("p k q -> p q k"))
+        word_win.append(load_words(2, sb.tile([P, T], I32, name="word_win2", align_bytes=64)))
+        c_raw = [load_chunk(0, shared_u, 4096)]
 
         def interleave(raw, name, copy):
             grouped = sb.tile([P, raw.shape[2], PACK], BF16, name=name, align_bytes=64)
-            copy(
-                grouped[:].rearrange("p (w e) i -> p w i e", e=4), raw[:].rearrange("p i (w e) -> p w i e", e=4)
-            )
+            copy(grouped[:].rearrange("p (w e) i -> p w i e", e=4), raw[:].rearrange("p i (w e) -> p w i e", e=4))
             return grouped
 
         def quantize(grouped, name):
@@ -102,54 +98,70 @@ def tile_list_tabts_gelu_kernel(tc, tab_words, tab_scales, w4_words, w4_scales, 
         def gather(dst, window, lo, hi):
             nc.vector.tensor_copy(dst, window.indirect(offsets[:, lo // 16 : hi // 16]))
 
-        picked = [sb.tile([P, S], U32, name=f"picked{a}", align_bytes=64) for a in range(PASSES - 1)]
-        picked_scales = sb.tile([P, S], U8, name="picked_scales", tag="picked_scales_then_bias", align_bytes=64)
+        picked_scales = sb.tile([P, S], U8, name="picked_scales", align_bytes=64)
         ts_picked = sb.tile([P, S], F32, name="ts_picked")
+        tab_planes = sb.tile([P, PASSES, S], U8, name="tab_planes", align_bytes=64)
 
-        gather(picked_scales[:], scale_win[:], 0, S)
-        for q in (0, 2, 1, 3):
-            nc.sync.dma_start(
-                tab_planes[32 * q : 32 * q + 4, :, :].bitcast(I32),
-                picked_scales[ROW0 + 12 * q : ROW0 + 12 * q + 12, :].bitcast(I32),
-            )
-        c_raw.append(load_rows(c[:, c_cuts[1][0] : c_cuts[1][1]], "c_raw1", "scales_then_c"))
-        gather(picked[0][:], word_win[0][:].bitcast(U32), 0, S)
-        c_raw.append(load_rows(c[:, c_cuts[2][0] : c_cuts[2][1]], "c_raw2", "words0_then_c"))
-        bias = sb.tile([P, 1], F32, name="bias", tag="picked_scales_then_bias", align_bytes=64)
-        nc.sync.dma_start(bias[:], b.rearrange("(p o) -> p o", o=1))
         gather(ts_picked[:], ts_win[:], 0, S)
-        u_codes, u_scales = quantize(interleave(u_raw, "u_bf", nc.scalar.copy), "u")
-        c_raw.append(load_rows(c[:, c_cuts[3][0] : c_cuts[3][1]], "c_raw3", "u_raw"))
-        gather(picked[1][:], word_win[1][:].bitcast(U32), 0, S)
-        c_q = [quantize(interleave(c_raw[0], "c_bf0", nc.scalar.copy), "c0")]
+        gather(picked_scales[:], scale_win[:], 0, S)
+        for r in range(4):
+            first = ROW0 + 3 * r
+            nc.sync.dma_start(
+                tab_planes[r:P:32, :, :].bitcast(I32), picked_scales[first : first + 45 : 4, :].bitcast(I32)
+            )
+        c_raw += [load_chunk(1, shared, 0), load_chunk(2, shared, 4096)]
+        u_bf = interleave(u_raw, "u_bf", nc.scalar.copy)
+
+        ts_cols = sb.tile([P, S // P], F32, name="ts_cols")
+        ts_rows = sb.tile([P, S], F32, name="ts_rows")
+        for g in range(2):
+            turned = ps.tile([P, 4, P], F32, name=f"turned{g}", tag=f"ts_bank{g}")
+            for k in range(4):
+                j0 = (4 * g + k) * P
+                nc.tensor.transpose(turned[:, k, :], ts_picked[:, j0 : j0 + P], ident[:])
+            nc.scalar.copy(ts_cols[:, 4 * g : 4 * g + 4], turned[:, :, TS_ROW])
+        for g in range(2):
+            spread = ps.tile([P, 4, P], F32, name=f"spread{g}", tag=f"ts_bank{g}")
+            for k in range(4):
+                col = 4 * g + k
+                nc.tensor.transpose(spread[:, k, :], ts_cols[:, col : col + 1].to_broadcast([P, P]), ident[:])
+            nc.scalar.copy(ts_rows[:, g * HALF : (g + 1) * HALF], spread[:].rearrange("p k q -> p (k q)"))
+
+        picked = [
+            shared_u.tile([P, S], U32, name="picked0", offset=0, align_bytes=64),
+            sb.tile([P, S], U32, name="picked1", align_bytes=64),
+        ]
         last = [sb.tile([P, HALF], U32, name=f"last{h}", align_bytes=64) for h in range(2)]
+        gather(picked[0][:], word_win[0][:].bitcast(U32), 0, S)
+        c_raw += [load_chunk(3, shared, WIN0), load_chunk(4, shared, WIN0 + 2048)]
+        u_codes, u_scales = quantize(u_bf, "u")
+        gather(picked[1][:], word_win[1][:].bitcast(U32), 0, S)
+        bias = sb.tile([P, 1], F32, name="bias", tag="words1_then_bias", align_bytes=64)
+        nc.sync.dma_start(bias[:], b.rearrange("(p o) -> p o", o=1))
         for h in range(2):
             gather(last[h][:], word_win[2][:].bitcast(U32), h * HALF, (h + 1) * HALF)
-        c_q.append(quantize(interleave(c_raw[1], "c_bf1", nc.scalar.copy), "c1"))
-        c_bf2 = interleave(c_raw[2], "c_bf2", nc.scalar.copy)
-        c_bf3 = interleave(c_raw[3], "c_bf3", nc.vector.tensor_copy)
-        c_q.append(quantize(c_bf2, "c2"))
-        c_q.append(quantize(c_bf3, "c3"))
+        c_bf = [interleave(c_raw[k], f"c_bf{k}", nc.scalar.copy) for k in range(4)]
+        c_q = [quantize(c_bf[k], f"c{k}") for k in range(3)]
+        c_bf.append(interleave(c_raw[4], "c_bf4", nc.vector.tensor_copy))
+        c_q += [quantize(c_bf[k], f"c{k}") for k in (3, 4)]
 
         acc = [ps.tile([P, hi - lo], F32, name=f"acc{lo}") for lo, hi in c_cuts]
 
         def table_pass(k, a):
             lo, hi = c_cuts[k]
-            step = 512 if hi - lo == 512 else 128
-            for n0 in range(lo, hi, step):
-                if a < PASSES - 1:
-                    words = picked[a][:, n0 : n0 + step]
-                else:
-                    words = last[n0 // HALF][:, n0 % HALF : n0 % HALF + step]
-                nc.tensor.matmul_mx(
-                    out=acc[k][:, n0 - lo : n0 - lo + step],
-                    lhsT=w4_codes[:, a, :].bitcast(FP4X4),
-                    lhsT_scale=w4_planes[:, a, :],
-                    rhs=words.bitcast(FP8X4),
-                    rhs_scale=tab_planes[:, a, n0 : n0 + step],
-                    start=(a == 0 and n0 == lo and k > 0),
-                    stop=(a == PASSES - 1 and k == 0),
-                )
+            if a < PASSES - 1:
+                words = picked[a][:, lo:hi]
+            else:
+                words = last[lo // HALF][:, lo % HALF : lo % HALF + hi - lo]
+            nc.tensor.matmul_mx(
+                out=acc[k][:],
+                lhsT=w4_codes[:, a, :].bitcast(FP4X4),
+                lhsT_scale=w4_planes[:, a, :],
+                rhs=words.bitcast(FP8X4),
+                rhs_scale=tab_planes[:, a, lo:hi],
+                start=(a == 0),
+                stop=False,
+            )
 
         def c_pass(k):
             nc.tensor.matmul_mx(
@@ -158,26 +170,26 @@ def tile_list_tabts_gelu_kernel(tc, tab_words, tab_scales, w4_words, w4_scales, 
                 lhsT_scale=u_scales[:],
                 rhs=c_q[k][0][:].bitcast(FP8X4),
                 rhs_scale=c_q[k][1][:],
-                start=(k == 0),
-                stop=(k > 0),
+                start=False,
+                stop=True,
             )
 
-        c_pass(0)
         for a in range(PASSES):
-            table_pass(0, a)
-        for a in range(PASSES - 1):
-            for k in range(1, 4):
+            for k in range(len(c_cuts)):
                 table_pass(k, a)
-        table_pass(1, PASSES - 1)
-        c_pass(1)
-        for k in range(2, 4):
-            table_pass(k, PASSES - 1)
-        for k in range(2, 4):
+        for k in range(len(c_cuts)):
             c_pass(k)
 
+        scaled = [
+            shared.tile([P, 256], F32, name="scaled0", offset=0, align_bytes=64),
+            shared.tile([P, 256], F32, name="scaled1", offset=4096, align_bytes=64),
+            shared.tile([P, 256], F32, name="scaled2", offset=WIN0, align_bytes=64),
+            sb.tile([P, 128], F32, name="scaled3"),
+            sb.tile([P, 128], F32, name="scaled4"),
+        ]
+        result = sb.tile([P, S], F32, name="result")
         for k, (lo, hi) in enumerate(c_cuts):
-            scaled = sb.tile([P, hi - lo], F32, name=f"scaled{k}", tag=("c_bf3" if k == 1 else f"scaled{k}"), align_bytes=64)
-            nc.vector.tensor_tensor(scaled[:], acc[k][:], ts_picked[:, lo:hi], MULT)
-            result = sb.tile([P, hi - lo], F32, name=f"result{k}")
-            nc.scalar.activation(result[:], scaled[:], GELU, bias=bias[:])
-            nc.sync.dma_start(out[:, lo:hi], result[:])
+            nc.vector.tensor_tensor(scaled[k][:], acc[k][:], ts_rows[:, lo:hi], MULT)
+            nc.scalar.activation(result[:, lo:hi], scaled[k][:], GELU, bias=bias[:])
+        for lo, hi in ((0, 512), (512, 768), (768, 1024)):
+            nc.sync.dma_start(out[:, lo:hi], result[:, lo:hi])

@@ -43,8 +43,7 @@ def tile_list_tabts_gelu_kernel(tc, tab_words, tab_scales, w4_words, w4_scales, 
         scale_win = shared.tile([P, T], U8, name="scale_win", offset=4096 - T // 2, align_bytes=64)
         nc.vector.memset(scale_win[:].bitcast(I32), 0)
         ts_win = sb.tile([P, T], F32, name="ts_win", align_bytes=64)
-        nc.vector.memset(ts_win[0:TS_ROW, 0 : T // 2].bitcast(I32), 0)
-        nc.gpsimd.memset(ts_win[0:TS_ROW, T // 2 : T].bitcast(I32), 0)
+        nc.vector.memset(ts_win[0:TS_ROW, :].bitcast(I32), 0)
         nc.scalar.dma_start(ts_win[TS_ROW:P, :], ts[0:1, :])
 
         ident = sb.tile([P, P], F32, name="ident")
@@ -131,17 +130,21 @@ def tile_list_tabts_gelu_kernel(tc, tab_words, tab_scales, w4_words, w4_scales, 
             shared_u.tile([P, S], U32, name="picked0", offset=0, align_bytes=64),
             sb.tile([P, S], U32, name="picked1", align_bytes=64),
         ]
-        last = [sb.tile([P, HALF], U32, name=f"last{h}", align_bytes=64) for h in range(2)]
+        last = [
+            sb.tile([P, HALF], U32, name="last0", align_bytes=64),
+            shared_u.tile([P, HALF], U32, name="last1", offset=4096, align_bytes=64),
+        ]
         gather(picked[0][:], word_win[0][:].bitcast(U32), 0, S)
         c_raw += [load_chunk(3, shared, WIN0), load_chunk(4, shared, WIN0 + 2048)]
         u_codes, u_scales = quantize(u_bf, "u")
         gather(picked[1][:], word_win[1][:].bitcast(U32), 0, S)
         bias = sb.tile([P, 1], F32, name="bias", tag="words1_then_bias", align_bytes=64)
         nc.sync.dma_start(bias[:], b.rearrange("(p o) -> p o", o=1))
-        for h in range(2):
-            gather(last[h][:], word_win[2][:].bitcast(U32), h * HALF, (h + 1) * HALF)
+        gather(last[0][:], word_win[2][:].bitcast(U32), 0, HALF)
         c_bf = [interleave(c_raw[k], f"c_bf{k}", nc.scalar.copy) for k in range(4)]
-        c_q = [quantize(c_bf[k], f"c{k}") for k in range(3)]
+        c_q = [quantize(c_bf[0], "c0")]
+        gather(last[1][:], word_win[2][:].bitcast(U32), HALF, S)
+        c_q += [quantize(c_bf[k], f"c{k}") for k in (1, 2)]
         c_bf.append(interleave(c_raw[4], "c_bf4", nc.vector.tensor_copy))
         c_q += [quantize(c_bf[k], f"c{k}") for k in (3, 4)]
 
@@ -174,10 +177,15 @@ def tile_list_tabts_gelu_kernel(tc, tab_words, tab_scales, w4_words, w4_scales, 
                 stop=True,
             )
 
-        for a in range(PASSES):
+        for a in range(PASSES - 1):
             for k in range(len(c_cuts)):
                 table_pass(k, a)
-        for k in range(len(c_cuts)):
+        for k in (0, 1):
+            table_pass(k, PASSES - 1)
+        c_pass(0)
+        for k in (2, 3, 4):
+            table_pass(k, PASSES - 1)
+        for k in (1, 2, 3, 4):
             c_pass(k)
 
         scaled = [

@@ -82,17 +82,19 @@ def tile_list_tabts_gelu_kernel(tc, tab_words, tab_scales, w4_words, w4_scales, 
         word_win.append(load_words(2, sb.tile([P, T], I32, name="word_win2", align_bytes=64)))
         c_raw = [load_chunk(0, shared_u, 4096)]
 
-        def interleave(raw, name, copy):
-            grouped = sb.tile([P, raw.shape[2], PACK], BF16, name=name, align_bytes=64)
-            copy(grouped[:].rearrange("p (w e) i -> p w i e", e=4), raw[:].rearrange("p i (w e) -> p w i e", e=4))
+        def interleave(raw, grouped, copy):
+            copy(grouped.rearrange("p (w e i) -> p w i e", e=4, i=PACK), raw.rearrange("p i (w e) -> p w i e", e=4))
             return grouped
 
+        def bf16_tile(name, width):
+            return sb.tile([P, PACK * width], BF16, name=name, align_bytes=64)
+
         def quantize(grouped, name):
-            width = grouped.shape[1]
+            width = grouped.shape[1] // PACK
             codes = sb.tile([P, width], U32, name=name + "_codes", align_bytes=64)
             scales = sb.tile([P, width], U8, name=name + "_scales", align_bytes=64)
-            nc.vector.quantize_mx(out=codes[:].bitcast(FP8X4), scales=scales[:], in_=grouped[:].rearrange("p w i -> p (w i)"))
-            return codes, scales
+            nc.vector.quantize_mx(out=codes[:].bitcast(FP8X4), scales=scales[:], in_=grouped)
+            return codes[:], scales[:]
 
         def gather(dst, window, lo, hi):
             nc.vector.tensor_copy(dst, window.indirect(offsets[:, lo // 16 : hi // 16]))
@@ -109,7 +111,8 @@ def tile_list_tabts_gelu_kernel(tc, tab_words, tab_scales, w4_words, w4_scales, 
                 tab_planes[r:P:32, :, :].bitcast(I32), picked_scales[first : first + 45 : 4, :].bitcast(I32)
             )
         c_raw += [load_chunk(1, shared, 0), load_chunk(2, shared, 4096)]
-        u_bf = interleave(u_raw, "u_bf", nc.scalar.copy)
+        u_c0_bf = bf16_tile("u_c0_bf", M + 256)
+        interleave(u_raw[:], u_c0_bf[:, 0 : PACK * M], nc.scalar.copy)
 
         ts_cols = sb.tile([P, S // P], F32, name="ts_cols")
         ts_rows = sb.tile([P, S], F32, name="ts_rows")
@@ -135,18 +138,21 @@ def tile_list_tabts_gelu_kernel(tc, tab_words, tab_scales, w4_words, w4_scales, 
             shared_u.tile([P, HALF], U32, name="last1", offset=4096, align_bytes=64),
         ]
         gather(picked[0][:], word_win[0][:].bitcast(U32), 0, S)
-        c_raw += [load_chunk(3, shared, WIN0), load_chunk(4, shared, WIN0 + 2048)]
-        u_codes, u_scales = quantize(u_bf, "u")
+        c_tail = shared.tile([P, PACK, 256], F32, name="c_tail", offset=WIN0, align_bytes=64)
+        load_rows(c[:, 768:S], c_tail)
         gather(picked[1][:], word_win[1][:].bitcast(U32), 0, S)
         bias = sb.tile([P, 1], F32, name="bias", tag="words1_then_bias", align_bytes=64)
         nc.sync.dma_start(bias[:], b.rearrange("(p o) -> p o", o=1))
         gather(last[0][:], word_win[2][:].bitcast(U32), 0, HALF)
-        c_bf = [interleave(c_raw[k], f"c_bf{k}", nc.scalar.copy) for k in range(4)]
-        c_q = [quantize(c_bf[0], "c0")]
+        interleave(c_raw[0][:], u_c0_bf[:, PACK * M :], nc.scalar.copy)
+        c_bf = [interleave(c_raw[k][:], bf16_tile(f"c_bf{k}", 256)[:], nc.scalar.copy) for k in (1, 2)]
+        c_bf4 = interleave(c_tail[:, :, 128:256], bf16_tile("c_bf4", 128)[:], nc.scalar.copy)
+        joint_codes, joint_scales = quantize(u_c0_bf[:], "u_c0")
+        u_codes, u_scales = joint_codes[:, 0:M], joint_scales[:, 0:M]
+        c_q = [(joint_codes[:, M:], joint_scales[:, M:])]
         gather(last[1][:], word_win[2][:].bitcast(U32), HALF, S)
-        c_q += [quantize(c_bf[k], f"c{k}") for k in (1, 2)]
-        c_bf.append(interleave(c_raw[4], "c_bf4", nc.vector.tensor_copy))
-        c_q += [quantize(c_bf[k], f"c{k}") for k in (3, 4)]
+        c_q += [quantize(c_bf[k - 1], f"c{k}") for k in (1, 2)]
+        c_bf3 = interleave(c_tail[:, :, 0:128], bf16_tile("c_bf3", 128)[:], nc.vector.tensor_copy)
 
         acc = [ps.tile([P, hi - lo], F32, name=f"acc{lo}") for lo, hi in c_cuts]
 
@@ -169,10 +175,10 @@ def tile_list_tabts_gelu_kernel(tc, tab_words, tab_scales, w4_words, w4_scales, 
         def c_pass(k):
             nc.tensor.matmul_mx(
                 out=acc[k][:],
-                lhsT=u_codes[:].bitcast(FP8X4),
-                lhsT_scale=u_scales[:],
-                rhs=c_q[k][0][:].bitcast(FP8X4),
-                rhs_scale=c_q[k][1][:],
+                lhsT=u_codes.bitcast(FP8X4),
+                lhsT_scale=u_scales,
+                rhs=c_q[k][0].bitcast(FP8X4),
+                rhs_scale=c_q[k][1],
                 start=False,
                 stop=True,
             )
@@ -185,7 +191,7 @@ def tile_list_tabts_gelu_kernel(tc, tab_words, tab_scales, w4_words, w4_scales, 
         c_pass(0)
         for k in (2, 3, 4):
             table_pass(k, PASSES - 1)
-        for k in (1, 2, 3, 4):
+        for k in (1, 2):
             c_pass(k)
 
         scaled = [
@@ -196,8 +202,19 @@ def tile_list_tabts_gelu_kernel(tc, tab_words, tab_scales, w4_words, w4_scales, 
             sb.tile([P, 128], F32, name="scaled4"),
         ]
         result = sb.tile([P, S], F32, name="result")
-        for k, (lo, hi) in enumerate(c_cuts):
+
+        def finish(k):
+            lo, hi = c_cuts[k]
             nc.vector.tensor_tensor(scaled[k][:], acc[k][:], ts_rows[:, lo:hi], MULT)
             nc.scalar.activation(result[:, lo:hi], scaled[k][:], GELU, bias=bias[:])
-        for lo, hi in ((0, 512), (512, 768), (768, 1024)):
+
+        for k in (0, 1):
+            finish(k)
+        c_q += [quantize(c_bf3, "c3"), quantize(c_bf4, "c4")]
+        for k in (3, 4):
+            c_pass(k)
+        for k in (2, 3, 4):
+            finish(k)
+        for lo, hi in ((0, 512), (512, 768), (768, 896)):
             nc.sync.dma_start(out[:, lo:hi], result[:, lo:hi])
+        nc.scalar.dma_start(out[:, 896:S], result[:, 896:S])

@@ -67,18 +67,23 @@ def tile_list_tabts_gelu_kernel(tc, tab_words, tab_scales, w4_words, w4_scales, 
         w4_planes = sb.tile([P, PASSES, M], U8, name="w4_planes", align_bytes=64)
         w4_codes = sb.tile([P, PASSES, 2 * M], U8, name="w4_codes", align_bytes=64)
 
-        word_win = [load_words(0, shared.tile([P, T], I32, name="word_win0", offset=WIN0, align_bytes=64))]
-        for a in range(PASSES):
-            first = ROW0 + 4 * a
-            nc.sync.dma_start(scale_win[first : first + 46 : 3, :].bitcast(I32), tab_scales[a].bitcast(I32))
-        u_raw = load_rows(u, shared_u.tile([P, PACK, M], F32, name="u_raw", offset=0, align_bytes=64))
-        nc.sync.dma_start(w4_codes[:].bitcast(I32), w4_words.rearrange("a p n -> p a n").bitcast(I32))
-        word_win.append(load_words(1, sb.tile([P, T], I32, name="word_win1", tag="words1_then_bias", align_bytes=64)))
-        for q in range(QUADS):
+        def load_w4_plane_rows(q):
             nc.sync.dma_start(
                 w4_planes[32 * q : 32 * q + 4, :, :].bitcast(I32),
                 w4_scales[:, 4 * q : 4 * q + 4, :].rearrange("a r n -> r a n").bitcast(I32),
             )
+
+        word_win = [load_words(0, shared.tile([P, T], I32, name="word_win0", offset=WIN0, align_bytes=64))]
+        for a in range(PASSES):
+            first = ROW0 + 4 * a
+            nc.sync.dma_start(scale_win[first : first + 46 : 3, :].bitcast(I32), tab_scales[a].bitcast(I32))
+        load_w4_plane_rows(0)
+        load_w4_plane_rows(1)
+        u_raw = load_rows(u, shared_u.tile([P, PACK, M], F32, name="u_raw", offset=0, align_bytes=64))
+        word_win.append(load_words(1, sb.tile([P, T], I32, name="word_win1", tag="words1_then_bias", align_bytes=64)))
+        nc.sync.dma_start(w4_codes[:].bitcast(I32), w4_words.rearrange("a p n -> p a n").bitcast(I32))
+        load_w4_plane_rows(2)
+        load_w4_plane_rows(3)
         word_win.append(load_words(2, sb.tile([P, T], I32, name="word_win2", align_bytes=64)))
         c_raw = [load_chunk(0, shared_u, 4096)]
 

@@ -46,10 +46,11 @@ def tile_list_tabts_gelu_kernel(tc, tab_words, tab_scales, w4_words, w4_scales, 
         nc.vector.memset(ts_win[0:TS_ROW, :].bitcast(I32), 0)
         nc.scalar.dma_start(ts_win[TS_ROW:P, :], ts[0:1, :])
 
+        warm = sb.tile([P, 2], F32, name="warm")
+        nc.gpsimd.memset(warm[:, 0:1], 0.0)
+        nc.scalar.activation(warm[:, 1:2], warm[:, 0:1], GELU)
         ident = sb.tile([P, P], F32, name="ident")
         make_identity(nc, ident[:])
-        warm = sb.tile([P, 1], F32, name="warm")
-        nc.scalar.activation(warm[:], ident[:, 0:1], GELU)
 
         def load_words(a, win):
             nc.sync.dma_start(win[:], tab_words[a].rearrange("p t i -> p (t i)").bitcast(I32))
@@ -73,17 +74,15 @@ def tile_list_tabts_gelu_kernel(tc, tab_words, tab_scales, w4_words, w4_scales, 
                 w4_scales[:, 4 * q : 4 * q + 4, :].rearrange("a r n -> r a n").bitcast(I32),
             )
 
-        word_win = [load_words(0, shared.tile([P, T], I32, name="word_win0", offset=WIN0, align_bytes=64))]
+        u_raw = load_rows(u, sb.tile([P, PACK, M], F32, name="u_raw", align_bytes=64))
+        nc.sync.dma_start(w4_codes[:].bitcast(I32), w4_words.rearrange("a p n -> p a n").bitcast(I32))
         for a in range(PASSES):
             first = ROW0 + 4 * a
             nc.sync.dma_start(scale_win[first : first + 46 : 3, :].bitcast(I32), tab_scales[a].bitcast(I32))
-        load_w4_plane_rows(0)
-        load_w4_plane_rows(1)
-        u_raw = load_rows(u, shared_u.tile([P, PACK, M], F32, name="u_raw", offset=0, align_bytes=64))
+        word_win = [load_words(0, shared.tile([P, T], I32, name="word_win0", offset=WIN0, align_bytes=64))]
+        for q in (2, 3, 0, 1):
+            load_w4_plane_rows(q)
         word_win.append(load_words(1, sb.tile([P, T], I32, name="word_win1", tag="words1_then_bias", align_bytes=64)))
-        nc.sync.dma_start(w4_codes[:].bitcast(I32), w4_words.rearrange("a p n -> p a n").bitcast(I32))
-        load_w4_plane_rows(2)
-        load_w4_plane_rows(3)
         word_win.append(load_words(2, sb.tile([P, T], I32, name="word_win2", align_bytes=64)))
         c_raw = [load_chunk(0, shared_u, 4096)]
 
@@ -135,7 +134,7 @@ def tile_list_tabts_gelu_kernel(tc, tab_words, tab_scales, w4_words, w4_scales, 
             nc.scalar.copy(ts_rows[:, g * HALF : (g + 1) * HALF], spread[:].rearrange("p k q -> p (k q)"))
 
         picked = [
-            shared_u.tile([P, S], U32, name="picked0", offset=0, align_bytes=64),
+            sb.tile([P, S], U32, name="picked0", align_bytes=64),
             sb.tile([P, S], U32, name="picked1", align_bytes=64),
         ]
         last = [

@@ -25,6 +25,7 @@ QUADS = 4
 ROW0 = 36
 WIN0 = 4 * T
 TS_ROW = P - 1
+VECTOR_SHARE = 64
 
 
 def tile_list_tabts_gelu_kernel(tc, tab_words, tab_scales, w4_words, w4_scales, c, u, ts, b, offs, out):
@@ -149,16 +150,12 @@ def tile_list_tabts_gelu_kernel(tc, tab_words, tab_scales, w4_words, w4_scales, 
         nc.sync.dma_start(bias[:], b.rearrange("(p o) -> p o", o=1))
         gather(last[0][:], word_win[2][:].bitcast(U32), 0, HALF)
         interleave(c_raw[0][:], u_c0_bf[:, PACK * M :], nc.scalar.copy)
-        c_bf = [interleave(c_raw[k][:], bf16_tile(f"c_bf{k}", 256)[:], nc.scalar.copy) for k in (1, 2)]
-        c_bf4 = interleave(c_tail[:, :, 128:256], bf16_tile("c_bf4", 128)[:], nc.scalar.copy)
         joint_codes, joint_scales = quantize(u_c0_bf[:], "u_c0")
         u_codes, u_scales = joint_codes[:, 0:M], joint_scales[:, 0:M]
         c_q = [(joint_codes[:, M:], joint_scales[:, M:])]
         gather(last[1][:], word_win[2][:].bitcast(U32), HALF, S)
-        c_q += [quantize(c_bf[k - 1], f"c{k}") for k in (1, 2)]
-        c_bf3 = interleave(c_tail[:, :, 0:128], bf16_tile("c_bf3", 128)[:], nc.vector.tensor_copy)
 
-        acc = [ps.tile([P, hi - lo], F32, name=f"acc{lo}") for lo, hi in c_cuts]
+        acc = {k: ps.tile([P, c_cuts[k][1] - c_cuts[k][0]], F32, name=f"acc{k}", tag=f"bank{k}") for k in (0, 1, 2, 4)}
 
         def table_pass(k, a):
             lo, hi = c_cuts[k]
@@ -187,38 +184,45 @@ def tile_list_tabts_gelu_kernel(tc, tab_words, tab_scales, w4_words, w4_scales, 
                 stop=True,
             )
 
-        for a in range(PASSES - 1):
-            for k in range(len(c_cuts)):
-                table_pass(k, a)
-        for k in (0, 1):
-            table_pass(k, PASSES - 1)
-        c_pass(0)
-        for k in (2, 3, 4):
-            table_pass(k, PASSES - 1)
-        for k in (1, 2):
-            c_pass(k)
+        scaled_first = sb.tile([P, 256], F32, name="scaled_first")
+        scaled_second = shared.tile([P, 256], F32, name="scaled_second", offset=4096, align_bytes=64)
+        scaled_rest = shared.tile([P, HALF], F32, name="scaled_rest", offset=WIN0, align_bytes=64)
+        scaled = [scaled_first[:], scaled_second[:], scaled_rest[:, 0:256], scaled_rest[:, 256:384], scaled_rest[:, 384:HALF]]
 
-        scaled = [
-            shared.tile([P, 256], F32, name="scaled0", offset=0, align_bytes=64),
-            shared.tile([P, 256], F32, name="scaled1", offset=4096, align_bytes=64),
-            shared.tile([P, 256], F32, name="scaled2", offset=WIN0, align_bytes=64),
-            sb.tile([P, 128], F32, name="scaled3"),
-            sb.tile([P, 128], F32, name="scaled4"),
-        ]
-        result = sb.tile([P, S], F32, name="result")
-
-        def finish(k):
+        def product(k):
             lo, hi = c_cuts[k]
-            nc.vector.tensor_tensor(scaled[k][:], acc[k][:], ts_rows[:, lo:hi], MULT)
-            nc.scalar.activation(result[:, lo:hi], scaled[k][:], GELU, bias=bias[:])
+            nc.vector.tensor_tensor(scaled[k], acc[k][:], ts_rows[:, lo:hi], MULT)
 
-        for k in (0, 1):
-            finish(k)
+        for a in range(PASSES):
+            for k in (0, 1):
+                table_pass(k, a)
+        c_pass(0)
+        for a in range(PASSES):
+            for k in (2, 4):
+                table_pass(k, a)
+        product(0)
+        c_q.append(quantize(interleave(c_raw[1][:], bf16_tile("c_bf1", 256)[:], nc.scalar.copy), "c1"))
+        c_pass(1)
+        acc[3] = ps.tile([P, 128], F32, name="acc3", tag="bank0")
+        for a in range(PASSES):
+            table_pass(3, a)
+        c_bf2 = bf16_tile("c_bf2", 256)
+        interleave(c_raw[2][:, :, 0:VECTOR_SHARE], c_bf2[:, 0 : PACK * VECTOR_SHARE], nc.vector.tensor_copy)
+        interleave(c_raw[2][:, :, VECTOR_SHARE:256], c_bf2[:, PACK * VECTOR_SHARE :], nc.scalar.copy)
+        c_q.append(quantize(c_bf2[:], "c2"))
+        c_pass(2)
+        c_bf3 = interleave(c_tail[:, :, 0:128], bf16_tile("c_bf3", 128)[:], nc.vector.tensor_copy)
+        product(1)
+        c_bf4 = interleave(c_tail[:, :, 128:256], bf16_tile("c_bf4", 128)[:], nc.scalar.copy)
         c_q += [quantize(c_bf3, "c3"), quantize(c_bf4, "c4")]
         for k in (3, 4):
             c_pass(k)
         for k in (2, 3, 4):
-            finish(k)
+            product(k)
+
+        result = sb.tile([P, S], F32, name="result")
+        for k, (lo, hi) in enumerate(c_cuts):
+            nc.scalar.activation(result[:, lo:hi], scaled[k], GELU, bias=bias[:])
         for lo, hi in ((0, 512), (512, 768), (768, 896)):
             nc.sync.dma_start(out[:, lo:hi], result[:, lo:hi])
         nc.scalar.dma_start(out[:, 896:S], result[:, 896:S])

from contextlib import ExitStack

import concourse.mybir as mybir
from concourse.masks import make_identity

K, M, T, S, L = 1536, 128, 2048, 1024, 512
FLOPS = 2 * (K + L) * M * S

F32 = mybir.dt.float32
BF16 = mybir.dt.bfloat16
I32 = mybir.dt.int32
U32 = mybir.dt.uint32
U16 = mybir.dt.uint16
U8 = mybir.dt.uint8
FP8X4 = mybir.dt.float8_e4m3fn_x4
FP4X4 = mybir.dt.float4_e2m1fn_x4
MULT = mybir.AluOpType.mult
GELU = mybir.ActivationFunctionType.Gelu_apprx_tanh

P = 128
PACK = 4
PASSES = K // (P * PACK)
HALF = S // 2
QUADS = 4
ROW0 = 36
WIN0 = 4 * T
TS_ROW = P - 1
VECTOR_SHARE = 64


def tile_list_tabts_gelu_kernel(tc, tab_words, tab_scales, w4_words, w4_scales, c, u, ts, b, offs, out):
    nc = tc.nc
    with ExitStack() as ctx:
        sb = ctx.enter_context(tc.tile_pool(name="sb", bufs=1))
        shared = ctx.enter_context(tc.tile_pool(name="shared", bufs=1))
        shared_u = ctx.enter_context(tc.tile_pool(name="shared_u", bufs=1))
        ps = ctx.enter_context(tc.psum_pool(name="ps", bufs=1))

        c_cuts = [(0, 256), (256, 512), (512, 768), (768, 896), (896, 1024)]

        offsets = sb.tile([P, S // 16], U16, name="offsets")
        nc.sync.dma_start(offsets[:], offs)

        scale_win = shared.tile([P, T], U8, name="scale_win", offset=4096 - T // 2, align_bytes=64)
        nc.vector.memset(scale_win[:].bitcast(I32), 0)
        ts_win = sb.tile([P, T], F32, name="ts_win", align_bytes=64)
        nc.vector.memset(ts_win[0:TS_ROW, :].bitcast(I32), 0)
        nc.scalar.dma_start(ts_win[TS_ROW:P, :], ts[0:1, :])

        warm = sb.tile([P, 2], F32, name="warm")
        nc.gpsimd.memset(warm[:, 0:1], 0.0)
        nc.scalar.activation(warm[:, 1:2], warm[:, 0:1], GELU)
        ident = sb.tile([P, P], F32, name="ident")
        make_identity(nc, ident[:])

        def load_words(a, win):
            nc.sync.dma_start(win[:], tab_words[a].rearrange("p t i -> p (t i)").bitcast(I32))
            return win

        def load_rows(rows, raw):
            nc.sync.dma_start(raw[:], rows.rearrange("(p i) w -> p i w", i=PACK))
            return raw

        def load_chunk(k, pool, offset):
            lo, hi = c_cuts[k]
            raw = pool.tile([P, PACK, hi - lo], F32, name=f"c_raw{k}", offset=offset, align_bytes=64)
            return load_rows(c[:, lo:hi], raw)

        w4_planes = sb.tile([P, PASSES, M], U8, name="w4_planes", align_bytes=64)
        w4_codes = sb.tile([P, PASSES, 2 * M], U8, name="w4_codes", align_bytes=64)

        def load_w4_plane_rows(q):
            nc.sync.dma_start(
                w4_planes[32 * q : 32 * q + 4, :, :].bitcast(I32),
                w4_scales[:, 4 * q : 4 * q + 4, :].rearrange("a r n -> r a n").bitcast(I32),
            )

        u_raw = load_rows(u, sb.tile([P, PACK, M], F32, name="u_raw", align_bytes=64))
        nc.sync.dma_start(w4_codes[:].bitcast(I32), w4_words.rearrange("a p n -> p a n").bitcast(I32))
        for a in range(PASSES):
            first = ROW0 + 4 * a
            nc.sync.dma_start(scale_win[first : first + 46 : 3, :].bitcast(I32), tab_scales[a].bitcast(I32))
        word_win = [load_words(0, shared.tile([P, T], I32, name="word_win0", offset=WIN0, align_bytes=64))]
        for q in (2, 3, 0, 1):
            load_w4_plane_rows(q)
        word_win.append(load_words(1, sb.tile([P, T], I32, name="word_win1", tag="words1_then_bias", align_bytes=64)))
        word_win.append(load_words(2, sb.tile([P, T], I32, name="word_win2", align_bytes=64)))
        c_raw = [load_chunk(0, shared_u, 4096)]

        def interleave(raw, grouped, copy):
            copy(grouped.rearrange("p (w e i) -> p w i e", e=4, i=PACK), raw.rearrange("p i (w e) -> p w i e", e=4))
            return grouped

        def bf16_tile(name, width):
            return sb.tile([P, PACK * width], BF16, name=name, align_bytes=64)

        def quantize(grouped, name):
            width = grouped.shape[1] // PACK
            codes = sb.tile([P, width], U32, name=name + "_codes", align_bytes=64)
            scales = sb.tile([P, width], U8, name=name + "_scales", align_bytes=64)
            nc.vector.quantize_mx(out=codes[:].bitcast(FP8X4), scales=scales[:], in_=grouped)
            return codes[:], scales[:]

        def gather(dst, window, lo, hi):
            nc.vector.tensor_copy(dst, window.indirect(offsets[:, lo // 16 : hi // 16]))

        picked_scales = sb.tile([P, S], U8, name="picked_scales", align_bytes=64)
        ts_picked = sb.tile([P, S], F32, name="ts_picked")
        tab_planes = sb.tile([P, PASSES, S], U8, name="tab_planes", align_bytes=64)

        gather(ts_picked[:], ts_win[:], 0, S)
        gather(picked_scales[:], scale_win[:], 0, S)
        for r in range(4):
            first = ROW0 + 3 * r
            nc.sync.dma_start(
                tab_planes[r:P:32, :, :].bitcast(I32), picked_scales[first : first + 45 : 4, :].bitcast(I32)
            )
        c_raw += [load_chunk(1, shared, 0), load_chunk(2, shared, 4096)]
        u_c0_bf = bf16_tile("u_c0_bf", M + 256)
        interleave(u_raw[:], u_c0_bf[:, 0 : PACK * M], nc.scalar.copy)

        ts_cols = sb.tile([P, S // P], F32, name="ts_cols")
        ts_rows = sb.tile([P, S], F32, name="ts_rows")
        for g in range(2):
            turned = ps.tile([P, 4, P], F32, name=f"turned{g}", tag=f"ts_bank{g}")
            for k in range(4):
                j0 = (4 * g + k) * P
                nc.tensor.transpose(turned[:, k, :], ts_picked[:, j0 : j0 + P], ident[:])
            nc.scalar.copy(ts_cols[:, 4 * g : 4 * g + 4], turned[:, :, TS_ROW])
        for g in range(2):
            spread = ps.tile([P, 4, P], F32, name=f"spread{g}", tag=f"ts_bank{g}")
            for k in range(4):
                col = 4 * g + k
                nc.tensor.transpose(spread[:, k, :], ts_cols[:, col : col + 1].to_broadcast([P, P]), ident[:])
            nc.scalar.copy(ts_rows[:, g * HALF : (g + 1) * HALF], spread[:].rearrange("p k q -> p (k q)"))

        picked = [
            sb.tile([P, S], U32, name="picked0", align_bytes=64),
            sb.tile([P, S], U32, name="picked1", align_bytes=64),
        ]
        last = [
            sb.tile([P, HALF], U32, name="last0", align_bytes=64),
            shared_u.tile([P, HALF], U32, name="last1", offset=4096, align_bytes=64),
        ]
        gather(picked[0][:], word_win[0][:].bitcast(U32), 0, S)
        c_tail = shared.tile([P, PACK, 256], F32, name="c_tail", offset=WIN0, align_bytes=64)
        load_rows(c[:, 768:S], c_tail)
        gather(picked[1][:], word_win[1][:].bitcast(U32), 0, S)
        bias = sb.tile([P, 1], F32, name="bias", tag="words1_then_bias", align_bytes=64)
        nc.sync.dma_start(bias[:], b.rearrange("(p o) -> p o", o=1))
        gather(last[0][:], word_win[2][:].bitcast(U32), 0, HALF)
        interleave(c_raw[0][:], u_c0_bf[:, PACK * M :], nc.scalar.copy)
        joint_codes, joint_scales = quantize(u_c0_bf[:], "u_c0")
        u_codes, u_scales = joint_codes[:, 0:M], joint_scales[:, 0:M]
        c_q = [(joint_codes[:, M:], joint_scales[:, M:])]
        gather(last[1][:], word_win[2][:].bitcast(U32), HALF, S)

        acc = {k: ps.tile([P, c_cuts[k][1] - c_cuts[k][0]], F32, name=f"acc{k}", tag=f"bank{k}") for k in (0, 1, 2, 4)}

        def table_pass(k, a):
            lo, hi = c_cuts[k]
            if a < PASSES - 1:
                words = picked[a][:, lo:hi]
            else:
                words = last[lo // HALF][:, lo % HALF : lo % HALF + hi - lo]
            nc.tensor.matmul_mx(
                out=acc[k][:],
                lhsT=w4_codes[:, a, :].bitcast(FP4X4),
                lhsT_scale=w4_planes[:, a, :],
                rhs=words.bitcast(FP8X4),
                rhs_scale=tab_planes[:, a, lo:hi],
                start=(a == 0),
                stop=False,
            )

        def c_pass(k):
            nc.tensor.matmul_mx(
                out=acc[k][:],
                lhsT=u_codes.bitcast(FP8X4),
                lhsT_scale=u_scales,
                rhs=c_q[k][0].bitcast(FP8X4),
                rhs_scale=c_q[k][1],
                start=False,
                stop=True,
            )

        scaled_first = sb.tile([P, 256], F32, name="scaled_first")
        scaled_second = shared.tile([P, 256], F32, name="scaled_second", offset=4096, align_bytes=64)
        scaled_rest = shared.tile([P, HALF], F32, name="scaled_rest", offset=WIN0, align_bytes=64)
        scaled = [scaled_first[:], scaled_second[:], scaled_rest[:, 0:256], scaled_rest[:, 256:384], scaled_rest[:, 384:HALF]]

        def product(k):
            lo, hi = c_cuts[k]
            nc.vector.tensor_tensor(scaled[k], acc[k][:], ts_rows[:, lo:hi], MULT)

        for a in range(PASSES):
            for k in (0, 1):
                table_pass(k, a)
        c_pass(0)
        for a in range(PASSES):
            for k in (2, 4):
                table_pass(k, a)
        product(0)
        c_q.append(quantize(interleave(c_raw[1][:], bf16_tile("c_bf1", 256)[:], nc.scalar.copy), "c1"))
        c_pass(1)
        acc[3] = ps.tile([P, 128], F32, name="acc3", tag="bank0")
        for a in range(PASSES):
            table_pass(3, a)
        c_bf2 = bf16_tile("c_bf2", 256)
        interleave(c_raw[2][:, :, 0:VECTOR_SHARE], c_bf2[:, 0 : PACK * VECTOR_SHARE], nc.vector.tensor_copy)
        interleave(c_raw[2][:, :, VECTOR_SHARE:256], c_bf2[:, PACK * VECTOR_SHARE :], nc.scalar.copy)
        c_q.append(quantize(c_bf2[:], "c2"))
        c_pass(2)
        c_bf3 = interleave(c_tail[:, :, 0:128], bf16_tile("c_bf3", 128)[:], nc.vector.tensor_copy)
        product(1)
        c_bf4 = interleave(c_tail[:, :, 128:256], bf16_tile("c_bf4", 128)[:], nc.scalar.copy)
        c_q += [quantize(c_bf3, "c3"), quantize(c_bf4, "c4")]
        for k in (3, 4):
            c_pass(k)
        for k in (2, 3, 4):
            product(k)

        result = sb.tile([P, S], F32, name="result")
        for k, (lo, hi) in enumerate(c_cuts):
            nc.scalar.activation(result[:, lo:hi], scaled[k], GELU, bias=bias[:])
        for lo, hi in ((0, 512), (512, 768), (768, 896)):
            nc.sync.dma_start(out[:, lo:hi], result[:, lo:hi])
        nc.scalar.dma_start(out[:, 896:S], result[:, 896:S])
